import numpy as np, ml_dtypes
CORES = [0,9,18,27,36,45,54,63,64,73,82,91,100,109,118,127]
N = 16
def setup_inputs(rng):
    return {"x": rng.standard_normal((N, 128, 16), dtype=np.float32).astype(ml_dtypes.bfloat16)}
def reference(x):
    b = 16 // N
    blocks = x.reshape(N, 128, N, b)
    return {"y": np.ascontiguousarray(blocks.transpose(2, 1, 0, 3)).reshape(N, 128, 16)}

@@ -1,0 +1,86 @@
+from concourse.bass import DstId, RemoteDMATransfer
+
+SCRATCH = {
+    "xs": ("sbuf", [128, 16], "bfloat16"),
+    "land": ("sbuf", [128, 16], "bfloat16"),
+}
+SEMAPHORES = ["loaded", "got", "sent", "arrived", "stored"]
+
+
+def bits(m):
+    return bin(m).count("1")
+
+
+def chip_plan(i, cores, topo):
+    n = len(cores)
+    me = cores[i]
+    base = topo.chip(me) * 8
+    par = topo.chip(me) & 1
+    team = [base + k for k in range(8)]
+    rot = [(i + t) % n for t in range(1, n)]
+    cross = [j for j in rot if (topo.chip(cores[j]) & 1) != par]
+    same = [j for j in rot if (topo.chip(cores[j]) & 1) == par]
+    cap = [c for c in team if topo.may_write(c, cores[cross[0]])]
+    non = [c for c in team if c not in cap]
+    jobs = {c: [] for c in team}
+    for d in (0, 1):
+        cd = [c for c in cap if topo.die(c) == d]
+        for t, j in enumerate([j for j in cross if topo.die(cores[j]) == d]):
+            jobs[cd[t % len(cd)]].append(j)
+        nd = [c for c in non if topo.die(c) == d and c != me] + [c for c in non if topo.die(c) == d and c == me]
+        for t, j in enumerate([j for j in same if topo.die(cores[j]) == d]):
+            jobs[nd[t % len(nd)]].append(j)
+    plan = {}
+    for c in team:
+        if len(jobs[c]) == 1:
+            plan[c] = [(jobs[c][0], 0x00FF)]
+        else:
+            plan[c] = [(jobs[c][0], 0x000F), (jobs[c][1], 0x00F0)]
+    near = [c for c in non if c != me and topo.die(c) == topo.die(me)]
+    near.sort(key=lambda c: len(jobs[c]))
+    plan[near[0]].append((i, 0xFF00))
+    return plan
+
+
+def rank_program(g, core, T, topo):
+    cores = list(T.cores)
+    n = len(cores)
+    owner = [i for i in range(n) if topo.chip(cores[i]) == topo.chip(core)][0]
+    me = cores[owner]
+    plan = chip_plan(owner, cores, topo)
+    sem = T.sem
+
+    def dst_id(c):
+        rid, pid, _se = topo.addr(c)
+        return DstId(rid=rid, pnc=pid)
+
+    def send_columns():
+        trs = [RemoteDMATransfer(dst_ids=[dst_id(cores[j])], dma_engine_mask=m, remote_sem=sem.arrived,
+                                 src=T.xs[:, j:j + 1], dst=T.land[:, owner:owner + 1])
+               for j, m in plan[core]]
+        g.remote_dma_fused(trs, local_sem=sem.sent)
+        return sum(bits(m) for _j, m in plan[core])
+
+    if core != me:
+        g.wait_ge(sem.got, 16)
+        left = send_columns()
+        g.wait_ge(sem.sent, left)
+        return
+
+    g.sync.dma_start(T.xs[:], T.x[:]).then_inc(sem.loaded, 16)
+    g.wait_ge(sem.loaded, 16)
+    mates = [c for c in plan if c != me]
+    g.remote_dma_fused([RemoteDMATransfer(dst_ids=[dst_id(c) for c in mates], dma_engine_mask=0xFFFF,
+                                          remote_sem=sem.got, srcs=[T.xs[:]], dsts=[T.xs[:] for _c in mates])],
+                       local_sem=sem.sent)
+    left = 16 + send_columns()
+
+    total = 0
+    for i in range(n):
+        for _c, lst in chip_plan(i, cores, topo).items():
+            total += sum(bits(m) for j, m in lst if j == owner)
+    g.sync.wait_ge(sem.arrived, total)
+    g.sync.dma_start(T.y[:], T.land[:]).then_inc(sem.stored, 16)
+    g.wait_ge(sem.sent, left)
+    g.wait_ge(sem.arrived, total)
+    g.wait_ge(sem.stored, 16)

@@ -27,7 +27,7 @@ def chip_plan(i, cores, topo):
         cd = [c for c in cap if topo.die(c) == d]
         for t, j in enumerate([j for j in cross if topo.die(cores[j]) == d]):
             jobs[cd[t % len(cd)]].append(j)
-        nd = [c for c in non if topo.die(c) == d and c != me] + [c for c in non if topo.die(c) == d and c == me]
+        nd = [c for c in non if topo.die(c) == d and c == me] + [c for c in non if topo.die(c) == d and c != me]
         for t, j in enumerate([j for j in same if topo.die(cores[j]) == d]):
             jobs[nd[t % len(nd)]].append(j)
     plan = {}
@@ -39,7 +39,9 @@ def chip_plan(i, cores, topo):
     near = [c for c in non if c != me and topo.die(c) == topo.die(me)]
     near.sort(key=lambda c: len(jobs[c]))
     plan[near[0]].append((i, 0xFF00))
-    return plan
+    order = [c for c in cap if c != me] + [c for c in non if c != me and len(jobs[c]) == 2] \
+        + [c for c in non if c != me and len(jobs[c]) == 1]
+    return plan, order
 
 
 def rank_program(g, core, T, topo):
@@ -47,7 +49,7 @@ def rank_program(g, core, T, topo):
     n = len(cores)
     owner = [i for i in range(n) if topo.chip(cores[i]) == topo.chip(core)][0]
     me = cores[owner]
-    plan = chip_plan(owner, cores, topo)
+    plan, mates = chip_plan(owner, cores, topo)
     sem = T.sem
 
     def dst_id(c):
@@ -69,7 +71,6 @@ def rank_program(g, core, T, topo):
 
     g.sync.dma_start(T.xs[:], T.x[:]).then_inc(sem.loaded, 16)
     g.wait_ge(sem.loaded, 16)
-    mates = [c for c in plan if c != me]
     g.remote_dma_fused([RemoteDMATransfer(dst_ids=[dst_id(c) for c in mates], dma_engine_mask=0xFFFF,
                                           remote_sem=sem.got, srcs=[T.xs[:]], dsts=[T.xs[:] for _c in mates])],
                        local_sem=sem.sent)
@@ -77,7 +78,7 @@ def rank_program(g, core, T, topo):
 
     total = 0
     for i in range(n):
-        for _c, lst in chip_plan(i, cores, topo).items():
+        for _c, lst in chip_plan(i, cores, topo)[0].items():
             total += sum(bits(m) for j, m in lst if j == owner)
     g.sync.wait_ge(sem.arrived, total)
     g.sync.dma_start(T.y[:], T.land[:]).then_inc(sem.stored, 16)

@@ -1,14 +1,21 @@
 from concourse.bass import DstId, RemoteDMATransfer
 
 SCRATCH = {
+    "xd": ("dram", [128, 16], "bfloat16"),
     "xs": ("sbuf", [128, 16], "bfloat16"),
     "land": ("sbuf", [128, 16], "bfloat16"),
 }
-SEMAPHORES = ["loaded", "got", "sent", "arrived", "stored"]
+SEMAPHORES = ["loaded", "loaded2", "got", "sent", "arrived", "stored"]
 
 
 def bits(m):
     return bin(m).count("1")
+
+
+def masks(lst):
+    if len(lst) == 1:
+        return [(lst[0], 0x00FF)]
+    return [(lst[0], 0x000F), (lst[1], 0x00F0)]
 
 
 def chip_plan(i, cores, topo):
@@ -27,21 +34,17 @@ def chip_plan(i, cores, topo):
         cd = [c for c in cap if topo.die(c) == d]
         for t, j in enumerate([j for j in cross if topo.die(cores[j]) == d]):
             jobs[cd[t % len(cd)]].append(j)
-        nd = [c for c in non if topo.die(c) == d and c == me] + [c for c in non if topo.die(c) == d and c != me]
-        for t, j in enumerate([j for j in same if topo.die(cores[j]) == d]):
-            jobs[nd[t % len(nd)]].append(j)
-    plan = {}
-    for c in team:
-        if len(jobs[c]) == 1:
-            plan[c] = [(jobs[c][0], 0x00FF)]
-        else:
-            plan[c] = [(jobs[c][0], 0x000F), (jobs[c][1], 0x00F0)]
-    near = [c for c in non if c != me and topo.die(c) == topo.die(me)]
-    near.sort(key=lambda c: len(jobs[c]))
-    plan[near[0]].append((i, 0xFF00))
-    order = [c for c in cap if c != me] + [c for c in non if c != me and len(jobs[c]) == 2] \
-        + [c for c in non if c != me and len(jobs[c]) == 1]
-    return plan, order
+    cap_h = [c for c in cap if c != me]
+    non_h = [c for c in non if c != me]
+    rest = list(same)
+    if me in non:
+        jobs[me] = [rest.pop(0), rest.pop(0)]
+    for t, c in enumerate(non_h):
+        jobs[c] = [rest.pop(0)] if t >= len(non_h) - 2 else [rest.pop(0), rest.pop(0)]
+    plan = {c: [masks(jobs[c])] for c in team}
+    plan[cap_h[0]].append(masks(rest))
+    plan[non_h[-1]][0].append((i, 0xFF00))
+    return plan, cap_h + non_h
 
 
 def rank_program(g, core, T, topo):
@@ -57,11 +60,14 @@ def rank_program(g, core, T, topo):
         return DstId(rid=rid, pnc=pid)
 
     def send_columns():
-        trs = [RemoteDMATransfer(dst_ids=[dst_id(cores[j])], dma_engine_mask=m, remote_sem=sem.arrived,
-                                 src=T.xs[:, j:j + 1], dst=T.land[:, owner:owner + 1])
-               for j, m in plan[core]]
-        g.remote_dma_fused(trs, local_sem=sem.sent)
-        return sum(bits(m) for _j, m in plan[core])
+        left = 0
+        for call in plan[core]:
+            g.remote_dma_fused([RemoteDMATransfer(dst_ids=[dst_id(cores[j])], dma_engine_mask=m,
+                                                  remote_sem=sem.arrived, src=T.xs[:, j:j + 1],
+                                                  dst=T.land[:, owner:owner + 1]) for j, m in call],
+                               local_sem=sem.sent)
+            left += sum(bits(m) for _j, m in call)
+        return left
 
     if core != me:
         g.wait_ge(sem.got, 16)
@@ -69,17 +75,20 @@ def rank_program(g, core, T, topo):
         g.wait_ge(sem.sent, left)
         return
 
-    g.sync.dma_start(T.xs[:], T.x[:]).then_inc(sem.loaded, 16)
+    g.sync.dma_start(T.xd[:], T.x[:]).then_inc(sem.loaded, 16)
+    g.scalar.dma_start(T.xs[:], T.x[:]).then_inc(sem.loaded2, 16)
     g.wait_ge(sem.loaded, 16)
     g.remote_dma_fused([RemoteDMATransfer(dst_ids=[dst_id(c) for c in mates], dma_engine_mask=0xFFFF,
-                                          remote_sem=sem.got, srcs=[T.xs[:]], dsts=[T.xs[:] for _c in mates])],
+                                          remote_sem=sem.got, srcs=[T.xd[:]], dsts=[T.xs[:] for _c in mates])],
                        local_sem=sem.sent)
+    g.wait_ge(sem.loaded2, 16)
     left = 16 + send_columns()
 
     total = 0
     for i in range(n):
-        for _c, lst in chip_plan(i, cores, topo)[0].items():
-            total += sum(bits(m) for j, m in lst if j == owner)
+        for _c, calls in chip_plan(i, cores, topo)[0].items():
+            for call in calls:
+                total += sum(bits(m) for j, m in call if j == owner)
     g.sync.wait_ge(sem.arrived, total)
     g.sync.dma_start(T.y[:], T.land[:]).then_inc(sem.stored, 16)
     g.wait_ge(sem.sent, left)

@@ -23,28 +23,40 @@ def chip_plan(i, cores, topo):
     me = cores[i]
     base = topo.chip(me) * 8
     par = topo.chip(me) & 1
+    home = topo.die(me)
     team = [base + k for k in range(8)]
     rot = [(i + t) % n for t in range(1, n)]
     cross = [j for j in rot if (topo.chip(cores[j]) & 1) != par]
     same = [j for j in rot if (topo.chip(cores[j]) & 1) == par]
     cap = [c for c in team if topo.may_write(c, cores[cross[0]])]
-    non = [c for c in team if c not in cap]
-    jobs = {c: [] for c in team}
-    for d in (0, 1):
-        cd = [c for c in cap if topo.die(c) == d]
-        for t, j in enumerate([j for j in cross if topo.die(cores[j]) == d]):
-            jobs[cd[t % len(cd)]].append(j)
-    cap_h = [c for c in cap if c != me]
-    non_h = [c for c in non if c != me]
-    rest = list(same)
-    if me in non:
-        jobs[me] = [rest.pop(0), rest.pop(0)]
-    for t, c in enumerate(non_h):
-        jobs[c] = [rest.pop(0)] if t >= len(non_h) - 2 else [rest.pop(0), rest.pop(0)]
-    plan = {c: [masks(jobs[c])] for c in team}
-    plan[cap_h[0]].append(masks(rest))
-    plan[non_h[-1]][0].append((i, 0xFF00))
-    return plan, cap_h + non_h
+    mate = [j for j in cross if topo.mates(topo.chip(cores[j]), topo.chip(me))]
+    far = [j for j in cross if j not in mate]
+    far_r = [j for j in far if topo.die(cores[j]) == home]
+    far_o = [j for j in far if topo.die(cores[j]) != home]
+    same_r = [j for j in same if topo.die(cores[j]) == home]
+    same_o = [j for j in same if topo.die(cores[j]) != home]
+    cap_r = [c for c in cap if c != me and topo.die(c) == home]
+    cap_o = [c for c in cap if topo.die(c) != home]
+    non_r = [c for c in team if c not in cap and c != me and topo.die(c) == home]
+    non_o = [c for c in team if c not in cap and topo.die(c) != home]
+    plan = {}
+    plan[cap_r[0]] = [masks(far_r[0:2]), masks(mate)]
+    plan[cap_o[0]] = [masks(far_o[0:2]), masks(same_o[3:4])]
+    plan[cap_o[1]] = [masks(far_o[2:4])]
+    plan[non_o[0]] = [masks(same_o[0:2])]
+    plan[non_o[1]] = [masks(same_o[2:3])]
+    if me in cap:
+        plan[me] = [masks(far_r[2:3])]
+        plan[non_r[0]] = [masks(same_r[0:2])]
+        plan[non_r[1]] = [masks(same_r[2:3])]
+        order = [cap_r[0], cap_o[0], cap_o[1], non_o[0], non_r[0], non_o[1], non_r[1]]
+    else:
+        plan[cap_r[1]] = [masks(far_r[2:3])]
+        plan[me] = [masks(same_r[0:2])]
+        plan[non_r[0]] = [masks(same_r[2:3])]
+        order = [cap_r[0], cap_o[0], cap_o[1], cap_r[1], non_o[0], non_r[0], non_o[1]]
+    plan[order[-1]][0].append((i, 0xFF00))
+    return plan, order
 
 
 def rank_program(g, core, T, topo):

from concourse.bass import DstId, RemoteDMATransfer

SCRATCH = {
    "xd": ("dram", [128, 16], "bfloat16"),
    "xs": ("sbuf", [128, 16], "bfloat16"),
    "land": ("sbuf", [128, 16], "bfloat16"),
}
SEMAPHORES = ["loaded", "loaded2", "got", "sent", "arrived", "stored"]


def bits(m):
    return bin(m).count("1")


def masks(lst):
    if len(lst) == 1:
        return [(lst[0], 0x00FF)]
    return [(lst[0], 0x000F), (lst[1], 0x00F0)]


def chip_plan(i, cores, topo):
    n = len(cores)
    me = cores[i]
    base = topo.chip(me) * 8
    par = topo.chip(me) & 1
    home = topo.die(me)
    team = [base + k for k in range(8)]
    rot = [(i + t) % n for t in range(1, n)]
    cross = [j for j in rot if (topo.chip(cores[j]) & 1) != par]
    same = [j for j in rot if (topo.chip(cores[j]) & 1) == par]
    cap = [c for c in team if topo.may_write(c, cores[cross[0]])]
    mate = [j for j in cross if topo.mates(topo.chip(cores[j]), topo.chip(me))]
    far = [j for j in cross if j not in mate]
    far_r = [j for j in far if topo.die(cores[j]) == home]
    far_o = [j for j in far if topo.die(cores[j]) != home]
    same_r = [j for j in same if topo.die(cores[j]) == home]
    same_o = [j for j in same if topo.die(cores[j]) != home]
    cap_r = [c for c in cap if c != me and topo.die(c) == home]
    cap_o = [c for c in cap if topo.die(c) != home]
    non_r = [c for c in team if c not in cap and c != me and topo.die(c) == home]
    non_o = [c for c in team if c not in cap and topo.die(c) != home]
    plan = {}
    plan[cap_r[0]] = [masks(far_r[0:2]), masks(mate)]
    plan[cap_o[0]] = [masks(far_o[0:2]), masks(same_o[3:4])]
    plan[cap_o[1]] = [masks(far_o[2:4])]
    plan[non_o[0]] = [masks(same_o[0:2])]
    plan[non_o[1]] = [masks(same_o[2:3])]
    if me in cap:
        plan[me] = [masks(far_r[2:3])]
        plan[non_r[0]] = [masks(same_r[0:2])]
        plan[non_r[1]] = [masks(same_r[2:3])]
        order = [cap_r[0], cap_o[0], cap_o[1], non_o[0], non_r[0], non_o[1], non_r[1]]
    else:
        plan[cap_r[1]] = [masks(far_r[2:3])]
        plan[me] = [masks(same_r[0:2])]
        plan[non_r[0]] = [masks(same_r[2:3])]
        order = [cap_r[0], cap_o[0], cap_o[1], cap_r[1], non_o[0], non_r[0], non_o[1]]
    plan[order[-1]][0].append((i, 0xFF00))
    return plan, order


def rank_program(g, core, T, topo):
    cores = list(T.cores)
    n = len(cores)
    owner = [i for i in range(n) if topo.chip(cores[i]) == topo.chip(core)][0]
    me = cores[owner]
    plan, mates = chip_plan(owner, cores, topo)
    sem = T.sem

    def dst_id(c):
        rid, pid, _se = topo.addr(c)
        return DstId(rid=rid, pnc=pid)

    def send_columns():
        left = 0
        for call in plan[core]:
            g.remote_dma_fused([RemoteDMATransfer(dst_ids=[dst_id(cores[j])], dma_engine_mask=m,
                                                  remote_sem=sem.arrived, src=T.xs[:, j:j + 1],
                                                  dst=T.land[:, owner:owner + 1]) for j, m in call],
                               local_sem=sem.sent)
            left += sum(bits(m) for _j, m in call)
        return left

    if core != me:
        g.wait_ge(sem.got, 16)
        left = send_columns()
        g.wait_ge(sem.sent, left)
        return

    g.sync.dma_start(T.xd[:], T.x[:]).then_inc(sem.loaded, 16)
    g.scalar.dma_start(T.xs[:], T.x[:]).then_inc(sem.loaded2, 16)
    g.wait_ge(sem.loaded, 16)
    g.remote_dma_fused([RemoteDMATransfer(dst_ids=[dst_id(c) for c in mates], dma_engine_mask=0xFFFF,
                                          remote_sem=sem.got, srcs=[T.xd[:]], dsts=[T.xs[:] for _c in mates])],
                       local_sem=sem.sent)
    g.wait_ge(sem.loaded2, 16)
    left = 16 + send_columns()

    total = 0
    for i in range(n):
        for _c, calls in chip_plan(i, cores, topo)[0].items():
            for call in calls:
                total += sum(bits(m) for j, m in call if j == owner)
    g.sync.wait_ge(sem.arrived, total)
    g.sync.dma_start(T.y[:], T.land[:]).then_inc(sem.stored, 16)
    g.wait_ge(sem.sent, left)
    g.wait_ge(sem.arrived, total)
    g.wait_ge(sem.stored, 16)
